import numpy as np
import ml_dtypes


def mxq(x, axis, fmt="e4m3"):
    dtype, down = {"e4m3": (ml_dtypes.float8_e4m3fn, 7), "e5m2": (ml_dtypes.float8_e5m2, 14)}[fmt]
    v = np.moveaxis(np.asarray(x, np.float32).astype(ml_dtypes.bfloat16).astype(np.float64), axis, -1)
    blocks = v.reshape(v.shape[:-1] + (-1, 32))
    amax = np.abs(blocks).max(-1, keepdims=True)
    byte = np.maximum(np.where(amax > 0, np.frexp(amax)[1] - 1 + 127, 0) - down, 1)
    scale = np.exp2(byte - 127.0)
    codes = (blocks / scale).astype(np.float32).astype(dtype).astype(np.float64)
    return np.moveaxis((codes * scale).reshape(v.shape), -1, axis)


WIDE = False


def mx_kscale(k):
    if not WIDE:
        return np.ones(k)
    levels = np.array([10, -10, 5, -5, 0])
    if k % 512:
        return np.exp2(np.random.permutation(np.resize(levels, k // 32))).repeat(32)
    a = np.empty((k // 512, 16))
    for p in range(k // 512):
        a[p, :8] = np.random.permutation(np.resize(levels, 8))
        for g in range(8):
            far = levels[np.abs(levels - a[p, g]) >= 10]
            a[p, g + 8] = far[np.random.randint(len(far))]
    return np.exp2(a.ravel()).repeat(32)


def f64(x):
    return np.asarray(x).astype(np.float64)


def striped8(idx):
    return np.asarray(idx).reshape(8, -1, 16).transpose(0, 2, 1).reshape(128, -1).astype(np.uint16)


def unstriped8(offs):
    return offs.reshape(8, 16, -1).transpose(0, 2, 1).reshape(8, -1).astype(np.int64)


def pick8(x, idx, run):
    r = np.arange(len(x))
    return x[r[:, None], idx[r % (8 * run) // run]]


E2M1 = np.array([0.0, 0.5, 1.0, 1.5, 2.0, 3.0, 4.0, 6.0, -0.0, -0.5, -1.0, -1.5, -2.0, -3.0, -4.0, -6.0])


def pack_weight(w, fmt):
    k, n = w.shape
    w = f64(np.asarray(w, np.float32).astype(ml_dtypes.bfloat16)).reshape(k // 32, 32, n)
    amax = np.abs(w).max(1)
    if fmt == "e4m3":
        byte = np.frexp(amax)[1] - 1 + 127 - 7
    else:
        mant, ex = np.frexp(amax / 6.0)
        byte = np.where(mant > 0.5, ex, ex - 1) + 127
    byte = np.clip(np.where(amax > 0, byte, 1), 1, 254)
    scaled = (w * np.exp2(127.0 - byte)[:, None, :]).reshape(k, n).astype(np.float32)
    by_word = np.ascontiguousarray(scaled.reshape(k // 512, 128, 4, n).transpose(0, 1, 3, 2))
    if fmt == "e4m3":
        words = by_word.astype(ml_dtypes.float8_e4m3fn).view(np.uint8)
    else:
        c = by_word.astype(ml_dtypes.float4_e2m1fn).view(np.uint8) & 0xF
        words = (c[..., 0::2] | (c[..., 1::2] << 4)).reshape(k // 512, 128, 2 * n)
    return np.ascontiguousarray(words), np.ascontiguousarray(byte.astype(np.uint8).reshape(k // 512, 16, n))


def unpack_weight(words, scales, fmt):
    g, _, n = scales.shape
    words = np.ascontiguousarray(words).reshape(g, 128, n, -1)
    if fmt == "e4m3":
        vals = words.view(ml_dtypes.float8_e4m3fn).astype(np.float64)
    else:
        nib = np.empty((g, 128, n, 4), np.uint8)
        nib[..., 0::2] = words & 0xF
        nib[..., 1::2] = words >> 4
        vals = E2M1[nib]
    vals = vals * np.repeat(np.exp2(scales.astype(np.float64) - 127.0), 8, axis=1)[..., None]
    return vals.transpose(0, 1, 3, 2).reshape(g * 512, n)


D, T, I, Q = 512, 1024, 512, 128


def setup_inputs():
    n = np.random.standard_normal
    idx = np.stack([np.random.permutation(T)[:I] for _ in range(8)])
    idx2 = np.stack([np.random.permutation(T)[:I] for _ in range(8)])
    idx3 = np.stack([np.random.permutation(T)[:I] for _ in range(8)])
    fd = mx_kscale(D)
    keysp = pack_weight(n((D, T)) / fd[:, None], "e2m1")
    return {
        "query": (n((D, Q)) * 0.9 / np.sqrt(D) * fd[:, None]).astype(np.float32),
        "query2": (n((D, Q)) * 0.9 / np.sqrt(D) * fd[:, None]).astype(np.float32),
        "keys_words": keysp[0],
        "keys_scales": keysp[1],
        "lam": (np.random.uniform(0.5, 1.3, (Q, 1))).astype(np.float32),
        "old": (1.0 * n((Q, T))).astype(np.float32),
        "offs": striped8(idx),
        "offs2": striped8(idx2),
        "offs3": striped8(idx3),
    }


def reference(query, query2, keys_words, keys_scales, lam, old, offs, offs2, offs3):
    idx = unstriped8(offs)
    idx2 = unstriped8(offs2)
    idx3 = unstriped8(offs3)
    keysu = unpack_weight(keys_words, keys_scales, "e2m1")
    queryq = mxq(f64(query), 0, "e4m3")
    a = queryq.T @ keysu
    query2q = mxq(f64(query2), 0, "e4m3")
    b = query2q.T @ keysu
    w = (np.maximum(pick8(a, idx, 16), pick8(b, idx2, 16)) - np.maximum(pick8(a, idx2, 16), pick8(b, idx, 16))) * f64(lam)
    f1 = np.zeros((Q, T))
    f1[np.arange(Q)[:, None], idx[np.arange(Q) % 128 // 16]] = w
    f2 = f1 + f64(old)
    y = pick8(f2, idx3, 16)
    return y

from contextlib import ExitStack

import concourse.mybir as mybir

D, T, I, Q = 512, 1024, 512, 128
FLOPS = 2 * 2 * D * Q * T

F32 = mybir.dt.float32
BF16 = mybir.dt.bfloat16
I32 = mybir.dt.int32
U32 = mybir.dt.uint32
U16 = mybir.dt.uint16
U8 = mybir.dt.uint8
FP8X4 = mybir.dt.float8_e4m3fn_x4
FP4X4 = mybir.dt.float4_e2m1fn_x4
ALU = mybir.AluOpType
COPY = mybir.ActivationFunctionType.Copy

P = 128
PACK = 4
N = 256
HALF = I // 2
LIST = 16


def tile_attend_exchanged_lean_through_heads_kernel(tc, query, query2, keys_words, keys_scales, lam, old, offs, offs2, offs3, out):
    nc = tc.nc
    with ExitStack() as ctx:
        keep = ctx.enter_context(tc.tile_pool(name="keep", bufs=1))
        psum = ctx.enter_context(tc.psum_pool(name="psum", bufs=1))

        idx = keep.tile([P, I // LIST], U16, name="idx")
        idx2 = keep.tile([P, I // LIST], U16, name="idx2")
        idx3 = keep.tile([P, I // LIST], U16, name="idx3")

        k_scales = keep.tile([P, T], U8, name="k_scales", align_bytes=64)

        raw = [keep.tile([P, PACK * Q], F32, name=f"raw{s}", tag=f"raw{s}") for s in range(2)]
        k_words = keep.tile([P, 2 * T], U8, name="k_words", align_bytes=64)
        nc.sync.dma_start(out=raw[0][:], in_=query.rearrange("(p j) q -> p (j q)", j=PACK))
        for quad in range(4):
            nc.sync.dma_start(
                out=k_scales[32 * quad : 32 * quad + 4, :].bitcast(I32),
                in_=keys_scales[0, 4 * quad : 4 * quad + 4, :].bitcast(I32),
            )
        nc.sync.dma_start(out=k_words[:].bitcast(I32), in_=keys_words[0].bitcast(I32))
        nc.sync.dma_start(out=raw[1][:], in_=query2.rearrange("(p j) q -> p (j q)", j=PACK))
        nc.sync.dma_start(idx[:], offs)
        nc.sync.dma_start(idx2[:], offs2)
        nc.sync.dma_start(idx3[:], offs3)

        f1 = keep.tile([P, T], F32, name="f1")
        nc.vector.memset(f1[:], 0.0)

        scores = []
        for s in range(2):
            grouped = keep.tile([P, Q * PACK], BF16, name=f"grouped{s}", tag=f"grouped{s}", align_bytes=64)
            for u in range(2):
                rows = slice(u * Q // 2, (u + 1) * Q // 2)
                nc.vector.tensor_copy(
                    out=grouped[:].rearrange("p (q j) -> p q j", j=PACK)[:, rows, :],
                    in_=raw[s][:].rearrange("p (j q) -> p q j", j=PACK)[:, rows, :],
                )
            codes = keep.tile([P, Q], U32, name=f"codes{s}", align_bytes=64)
            scales = keep.tile([P, Q], U8, name=f"scales{s}", align_bytes=64)
            for u in range(2):
                rows = slice(u * Q // 2, (u + 1) * Q // 2)
                nc.vector.quantize_mx(
                    out=codes[:, rows].bitcast(FP8X4),
                    scales=scales[:, rows],
                    in_=grouped[:, u * Q * PACK // 2 : (u + 1) * Q * PACK // 2],
                )
            score = keep.tile([P, T], F32, name=f"score{s}")
            for c in range(T // N):
                bank = psum.tile([P, N], F32, name=f"bank{s}_{c}")
                nc.tensor.matmul_mx(
                    out=bank[:],
                    lhsT=codes[:].bitcast(FP8X4),
                    lhsT_scale=scales[:],
                    rhs=k_words[:, 2 * N * c : 2 * N * (c + 1)].bitcast(FP4X4),
                    rhs_scale=k_scales[:, N * c : N * (c + 1)],
                    start=True,
                    stop=True,
                )
                nc.scalar.activation(score[:, N * c : N * (c + 1)], bank[:], COPY)
            scores.append(score)
        a, b = scores

        lam_col = keep.tile([P, 1], F32, name="lam_col", tag="grouped0", align_bytes=64)
        nc.sync.dma_start(out=lam_col[:], in_=lam)
        old_half = [
            keep.tile([P, T // 2], F32, name="old0", tag="raw1"),
            keep.tile([P, T // 2], F32, name="old1", tag="grouped1", align_bytes=64),
        ]
        for s in range(2):
            nc.sync.dma_start(out=old_half[s][:], in_=old[:, s * (T // 2) : (s + 1) * (T // 2)])

        lam_wide = keep.tile([P, HALF], F32, name="lam_wide")
        nc.vector.tensor_copy(out=lam_wide[:], in_=lam_col[:].to_broadcast([P, HALF]))

        def gather_vector(dst, window, offsets):
            nc.vector.tensor_copy(dst, window[:].indirect(offsets))

        def gather_scalar(dst, window, offsets):
            nc.scalar.activation(dst, window[:].indirect(offsets), COPY)

        picks = [keep.tile([P, HALF], F32, name=f"picked{h}") for h in range(2)]

        def pair(tile):
            return tile[:].rearrange("p (e i) -> p e i", e=2)

        for h in range(2):
            cols = slice(h * HALF // LIST, (h + 1) * HALF // LIST)
            first = gather_vector if h == 0 else gather_scalar
            ga = keep.tile([P, 2 * HALF], F32, name=f"ga{h}", tag="ga")
            gb = keep.tile([P, 2 * HALF], F32, name=f"gb{h}")
            first(gb[:, :HALF], b, idx2[:, cols])
            gather_scalar(gb[:, HALF:], b, idx[:, cols])
            first(ga[:, :HALF], a, idx[:, cols])
            first(ga[:, HALF:], a, idx2[:, cols])
            top = keep.tile([P, 2 * HALF], F32, name=f"top{h}")
            diff = keep.tile([P, HALF], F32, name=f"diff{h}")
            quarters = [slice(u * HALF // 2, (u + 1) * HALF // 2) for u in range(2)]
            for slots in quarters:
                nc.vector.tensor_tensor(pair(top)[:, :, slots], pair(ga)[:, :, slots], pair(gb)[:, :, slots], ALU.max)
            for slots in quarters:
                nc.vector.tensor_tensor(diff[:, slots], pair(top)[:, 0, slots], pair(top)[:, 1, slots], ALU.subtract)
            nc.vector.tensor_tensor(f1[:].indirect(idx[:, cols]), diff[:], lam_wide[:], ALU.mult)

        f2 = keep.tile([P, T], F32, name="f2")
        for s in range(2):
            cols = slice(s * (T // 2), (s + 1) * (T // 2))
            nc.vector.tensor_tensor(f2[:, cols], f1[:, cols], old_half[s][:], ALU.add)

        for h, gather, queue in ((0, gather_vector, nc.sync), (1, gather_scalar, nc.scalar)):
            picked = picks[h]
            gather(picked[:], f2, idx3[:, h * HALF // LIST : (h + 1) * HALF // LIST])
            queue.dma_start(out=out[:, h * HALF : (h + 1) * HALF], in_=picked[:])
